import numpy as np, ml_dtypes
CORES = [2,10,50,58,66,74,122]
N = 7
K, F = 2, 64
def setup_inputs(rng):
    return {"gr": rng.standard_normal((N, K, 128, N * F), dtype=np.float32).astype(ml_dtypes.bfloat16)}
def setup_inputs_big(rng):
    d = setup_inputs(rng)
    for k in ("gr",): d[k] = (d[k].astype(np.float32) * 1048576.0).astype(d[k].dtype)
    return d
def setup_inputs_small(rng):
    d = setup_inputs(rng)
    for k in ("gr",): d[k] = (d[k].astype(np.float32) * (1 / 1048576.0)).astype(d[k].dtype)
    return d
def reference(gr):
    s = gr.astype(np.float64).sum(axis=(0, 1))
    return {"y": np.stack([s[:, F * r:F * r + F] for r in range(N)]).astype(np.float32 if gr.dtype != np.float64 else np.float64)}

from concourse.bass import DstId, RemoteDMATransfer
from concourse.mybir import AluOpType

N, K, F = 7, 2, 64
CALLS = ((0,), (1,), (2,))

SCRATCH = {
    "t0": ("sbuf", [128, N * F], "bfloat16"),
    "t1": ("sbuf", [128, N * F], "bfloat16"),
    "ps": ("sbuf", [128, N * F], "float32"),
    "land": ("sbuf", [128, N * F], "float32"),
    "acc0": ("psum", [128, F], "float32"),
    "acc1": ("psum", [128, F], "float32"),
    "out": ("sbuf", [128, F], "float32"),
}
SEMAPHORES = ["vs", "done", "st", "sent"] + ["ld%d" % k for k in range(3)] \
    + ["pv%d" % k for k in range(len(CALLS))] + ["ar%d" % s for s in range(N)]


def _rounds(T, topo):
    n = len(T.cores)
    groups = []
    for r, c in enumerate(T.cores):
        for gp in groups:
            if any(topo.mates(topo.chip(c), topo.chip(T.cores[q])) for q in gp):
                gp.append(r)
                break
        else:
            groups.append([r])
    arr = list(range(len(groups))) + ([None] if len(groups) % 2 else [])
    m = len(arr)
    rounds = []
    for _ in range(m - 1):
        to = {}
        for i in range(m):
            x, y = arr[i], arr[m - 1 - i]
            if x is None:
                continue
            gx, gy = groups[x], (groups[y] if y is not None else [])
            for s in gx:
                to[s] = list(gy) + ([q for q in gx if q != s] if len(gy) < len(gx) else [])
        rounds.append(to)
        arr = [arr[0], arr[-1]] + arr[1:-1]
    rounds.reverse()
    for s in range(n):
        if sorted(d for to in rounds for d in to[s]) != [d for d in range(n) if d != s]:
            raise ValueError("the rounds do not serve every rank once")
    return rounds


def _plan(T, topo, rounds, r):
    src = T.cores[r]
    calls = []
    for ks in CALLS:
        ds = [d for k in ks for d in rounds[k][r]]
        common = topo.mask(src, T.cores[ds[0]])
        for d in ds:
            common &= topo.mask(src, T.cores[d])
        es = [b for b in range(common.bit_length()) if (common >> b) & 1]
        per = 1
        while per * 2 * len(ds) <= len(es):
            per *= 2
        call = []
        for j, d in enumerate(ds):
            if not topo.may_write(src, T.cores[d]):
                raise ValueError("rank %d may not write to rank %d" % (r, d))
            call.append((d, sum(1 << e for e in es[j * per:(j + 1) * per]), per))
        calls.append(call)
    return calls


def _runs(blocks):
    out = []
    for d in sorted(blocks):
        if out and out[-1][1] == d:
            out[-1][1] = d + 1
        else:
            out.append([d, d + 1])
    return [(a, b) for a, b in out]


def _hops(topo, a, b):
    ca, cb = topo.chip(a), topo.chip(b)
    if ca == cb:
        return 0
    return 1 if (topo.mates(ca, cb) or topo.same_plane(ca, cb)) else 2


def rank_program(g, core, T, topo):
    r = T.rank_of(core)
    if r is None:
        return
    n = len(T.cores)
    v = g.vector
    add = AluOpType.add
    rounds = _rounds(T, topo)
    calls = _plan(T, topo, rounds, r)
    need = [[d for d, _, _ in call] for call in calls] + [[r]]

    chunks = [(min(need[0]), max(need[0]) + 1)]
    left = _runs([d for d in range(n) if not chunks[0][0] <= d < chunks[0][1]])
    left.sort(key=lambda ab: min(i for i, ds in enumerate(need) if any(ab[0] <= d < ab[1] for d in ds)))
    chunks += left
    for c, (a, b) in enumerate(chunks):
        g.sync.dma_start(T.t0[:, a * F:b * F], T.gr[0, :, a * F:b * F]).then_inc(T.sem["ld%d" % c], 16)
        g.scalar.dma_start(T.t1[:, a * F:b * F], T.gr[1, :, a * F:b * F]).then_inc(T.sem["ld%d" % c], 16)
    here = set()

    def loaded(blocks):
        for c, (a, b) in enumerate(chunks):
            if c not in here and any(a <= d < b for d in blocks):
                v.wait_ge(T.sem["ld%d" % c], 32)
                here.add(c)

    sent = 0
    for k, call in enumerate(calls):
        loaded(need[k])
        runs = _runs(need[k])
        for a, b in runs:
            v.tensor_tensor(T.ps[:, a * F:b * F], T.t0[:, a * F:b * F], T.t1[:, a * F:b * F], add).then_inc(
                T.sem["pv%d" % k], 1)
        g.wait_ge(T.sem["pv%d" % k], len(runs))
        trs = []
        for d, mask, per in call:
            rid, pid, _ = topo.addr(T.cores[d])
            trs.append(RemoteDMATransfer(dst_ids=[DstId(rid=rid, pnc=pid)], dma_engine_mask=mask,
                                         remote_sem=T.sem["ar%d" % r],
                                         src=T.ps[:, d * F:(d + 1) * F], dst=T.land[:, r * F:(r + 1) * F]))
            sent += per
        g.remote_dma_fused(trs, local_sem=T.sem.sent)

    loaded(range(n))
    accs = (T.acc0, T.acc1)
    v.tensor_tensor(accs[0][:], T.t0[:, r * F:(r + 1) * F], T.t1[:, r * F:(r + 1) * F], add).then_inc(T.sem.vs, 1)
    due = []
    for s in range(n):
        if s == r:
            continue
        for k, call in enumerate(_plan(T, topo, rounds, s)):
            for d, _, per in call:
                if d == r:
                    due.append((k, _hops(topo, T.cores[s], core), s, per))
    due.sort()
    for i, (_, _, s, per) in enumerate(due):
        last = i == len(due) - 1
        v.wait_ge(T.sem["ar%d" % s], per)
        v.wait_ge(T.sem.vs, i + 1)
        dst = T.out if last else accs[(i + 1) % 2]
        v.tensor_tensor(dst[:], accs[i % 2][:], T.land[:, s * F:(s + 1) * F], add).then_inc(
            T.sem.done if last else T.sem.vs, 1)
    g.sync.wait_ge(T.sem.done, 1)
    g.sync.dma_start(T.y[:], T.out[:]).then_inc(T.sem.st, 16)
    g.sync.wait_ge(T.sem.st, 16)
    g.wait_ge(T.sem.sent, sent)
